import numpy as np
import ml_dtypes


def mxq(x, axis, fmt="e4m3"):
    dtype, down = {"e4m3": (ml_dtypes.float8_e4m3fn, 7), "e5m2": (ml_dtypes.float8_e5m2, 14)}[fmt]
    v = np.moveaxis(np.asarray(x, np.float32).astype(ml_dtypes.bfloat16).astype(np.float64), axis, -1)
    blocks = v.reshape(v.shape[:-1] + (-1, 32))
    amax = np.abs(blocks).max(-1, keepdims=True)
    byte = np.maximum(np.where(amax > 0, np.frexp(amax)[1] - 1 + 127, 0) - down, 1)
    scale = np.exp2(byte - 127.0)
    codes = (blocks / scale).astype(np.float32).astype(dtype).astype(np.float64)
    return np.moveaxis((codes * scale).reshape(v.shape), -1, axis)


WIDE = False


def mx_kscale(k):
    if not WIDE:
        return np.ones(k)
    levels = np.array([30, -30])
    if k % 512:
        return np.exp2(np.random.permutation(np.resize(levels, k // 32))).repeat(32)
    a = np.empty((k // 512, 16))
    for p in range(k // 512):
        a[p, :8] = np.random.permutation(np.resize(levels, 8))
        for g in range(8):
            far = levels[np.abs(levels - a[p, g]) >= 10]
            a[p, g + 8] = far[np.random.randint(len(far))]
    return np.exp2(a.ravel()).repeat(32)


def f64(x):
    return np.asarray(x).astype(np.float64)


def striped(idx):
    return np.tile(np.asarray(idx).reshape(-1, 16).T, (8, 1)).astype(np.uint16)


def unstriped(offs):
    return offs[:16].T.reshape(-1).astype(np.int64)


E2M1 = np.array([0.0, 0.5, 1.0, 1.5, 2.0, 3.0, 4.0, 6.0, -0.0, -0.5, -1.0, -1.5, -2.0, -3.0, -4.0, -6.0])


def pack_weight(w, fmt):
    k, n = w.shape
    w = f64(np.asarray(w, np.float32).astype(ml_dtypes.bfloat16)).reshape(k // 32, 32, n)
    amax = np.abs(w).max(1)
    if fmt in ("e4m3", "e5m2"):
        byte = np.frexp(amax)[1] - 1 + 127 - (7 if fmt == "e4m3" else 14)
    else:
        mant, ex = np.frexp(amax / 6.0)
        byte = np.where(mant > 0.5, ex, ex - 1) + 127
    byte = np.clip(np.where(amax > 0, byte, 1), 1, 254)
    scaled = (w * np.exp2(127.0 - byte)[:, None, :]).reshape(k, n).astype(np.float32)
    by_word = np.ascontiguousarray(scaled.reshape(k // 512, 128, 4, n).transpose(0, 1, 3, 2))
    if fmt in ("e4m3", "e5m2"):
        words = by_word.astype(ml_dtypes.float8_e4m3fn if fmt == "e4m3" else ml_dtypes.float8_e5m2).view(np.uint8)
    else:
        c = by_word.astype(ml_dtypes.float4_e2m1fn).view(np.uint8) & 0xF
        words = (c[..., 0::2] | (c[..., 1::2] << 4)).reshape(k // 512, 128, 2 * n)
    return np.ascontiguousarray(words), np.ascontiguousarray(byte.astype(np.uint8).reshape(k // 512, 16, n))


def unpack_weight(words, scales, fmt):
    g, _, n = scales.shape
    words = np.ascontiguousarray(words).reshape(g, 128, n, -1)
    if fmt in ("e4m3", "e5m2"):
        vals = words.view(ml_dtypes.float8_e4m3fn if fmt == "e4m3" else ml_dtypes.float8_e5m2).astype(np.float64)
    else:
        nib = np.empty((g, 128, n, 4), np.uint8)
        nib[..., 0::2] = words & 0xF
        nib[..., 1::2] = words >> 4
        vals = E2M1[nib]
    vals = vals * np.repeat(np.exp2(scales.astype(np.float64) - 127.0), 8, axis=1)[..., None]
    return vals.transpose(0, 1, 3, 2).reshape(g * 512, n)


def sigmoid(v):
    return 1.0 / (1.0 + np.exp(-v))


K, T, Z, J, R, O, N, L, E = 512, 1024, 1024, 256, 512, 128, 256, 512, 512


def setup_inputs():
    n = np.random.standard_normal
    idx = np.random.permutation(T)[:J]
    idx2 = np.random.permutation(Z)[:J]
    idx3 = np.random.permutation(J)[:O]
    idx4 = np.random.permutation(J)[:O]
    idx5 = np.random.permutation(E)[:O]
    fk = mx_kscale(K)
    fr = mx_kscale(R)
    fl = mx_kscale(L)
    xtp = pack_weight(n((K, T)) / fk[:, None], "e5m2")
    xop = pack_weight(n((K, Z)) / fk[:, None], "e4m3")
    wp = pack_weight(n((K, R)) * 1 / np.sqrt(K) * fk[:, None] * fr, "e2m1")
    wbp = pack_weight(n((R, N)) * 1 / np.sqrt(R) / fr[:, None], "e2m1")
    sxp = pack_weight(n((L, O)) / fl[:, None], "e4m3")
    wsp = pack_weight(n((L, N)) * 1 / np.sqrt(L) * fl[:, None], "e2m1")
    return {
        "xt_words": xtp[0],
        "xt_scales": xtp[1],
        "xo_words": xop[0],
        "xo_scales": xop[1],
        "w_words": wp[0],
        "w_scales": wp[1],
        "wb_words": wbp[0],
        "wb_scales": wbp[1],
        "sx_words": sxp[0],
        "sx_scales": sxp[1],
        "ws_words": wsp[0],
        "ws_scales": wsp[1],
        "tz": (n((N, E))).astype(np.float32),
        "so": (np.random.uniform(0.6, 1.6, (N, 1))).astype(np.float32),
        "bo": (np.random.uniform(-1.0, 1.0, (N, 1))).astype(np.float32),
        "offs": striped(idx),
        "offs2": striped(idx2),
        "offs3": striped(idx3),
        "offs4": striped(idx4),
        "offs5": striped(idx5),
    }


def reference(xt_words, xt_scales, xo_words, xo_scales, w_words, w_scales, wb_words, wb_scales, sx_words, sx_scales, ws_words, ws_scales, tz, so, bo, offs, offs2, offs3, offs4, offs5):
    idx = unstriped(offs)
    idx2 = unstriped(offs2)
    idx3 = unstriped(offs3)
    idx4 = unstriped(offs4)
    idx5 = unstriped(offs5)
    xtu = unpack_weight(xt_words, xt_scales, "e5m2")
    xou = unpack_weight(xo_words, xo_scales, "e4m3")
    wu = unpack_weight(w_words, w_scales, "e2m1")
    wbu = unpack_weight(wb_words, wb_scales, "e2m1")
    sxu = unpack_weight(sx_words, sx_scales, "e4m3")
    wsu = unpack_weight(ws_words, ws_scales, "e2m1")
    xtidxg = xtu[:, idx]
    a = wu.T @ xtidxg
    xoidx2g = xou[:, idx2]
    b = wu.T @ xoidx2g
    hid = np.abs(a[:, idx3] - b[:, idx4])
    hidq = mxq(hid, 0, "e4m3")
    p = wbu.T @ hidq + wsu.T @ sxu
    y = p * sigmoid(f64(tz)[:, idx5] * f64(so) + f64(bo))
    return y

@@ -1,0 +1,172 @@
+from contextlib import ExitStack
+
+import concourse.mybir as mybir
+
+K, T, Z, J, R, O, N, L, E = 512, 1024, 1024, 256, 512, 128, 256, 512, 512
+FLOPS = 2 * (2 * K * R * J + R * N * O + L * N * O)
+
+F32 = mybir.dt.float32
+BF16 = mybir.dt.bfloat16
+I32 = mybir.dt.int32
+U32 = mybir.dt.uint32
+U16 = mybir.dt.uint16
+U8 = mybir.dt.uint8
+E4M3 = mybir.dt.float8_e4m3fn_x4
+E5M2 = mybir.dt.float8_e5m2_x4
+E2M1 = mybir.dt.float4_e2m1fn_x4
+ACT = mybir.ActivationFunctionType
+ALU = mybir.AluOpType
+P = 128
+
+
+def tile_list_oneforboth_looked_skip_finalgate_kernel(
+    tc, xt_words, xt_scales, xo_words, xo_scales, w_words, w_scales, wb_words, wb_scales,
+    sx_words, sx_scales, ws_words, ws_scales, tz, so, bo, offs, offs2, offs3, offs4, offs5, out,
+):
+    nc = tc.nc
+    with ExitStack() as ctx:
+        lists = ctx.enter_context(tc.tile_pool(name="lists", bufs=1))
+        sb = ctx.enter_context(tc.tile_pool(name="sb", bufs=1))
+        ps = ctx.enter_context(tc.psum_pool(name="ps", bufs=1))
+
+        def tile(name, shape, dtype, tag=None):
+            return sb.tile(shape, dtype, name=name, tag=tag or name, align_bytes=64)
+
+        def load_list(name, src):
+            t = lists.tile(list(src.shape), U16, name=name)
+            nc.sync.dma_start(t[:], src)
+            return t
+
+        def load_words(queue, name, src):
+            t = tile(name, [P, src.shape[1] // 4], U32)
+            queue.dma_start(t[:].bitcast(I32), src.bitcast(I32))
+            return t
+
+        xt_s = tile("xt_s", [P, T], U8)
+        xo_s = tile("xo_s", [P, Z], U8)
+        w_s = tile("w_s", [P, R], U8)
+        late_s = tile("late_s", [P, 2 * N + O], U8)
+        wb_s, ws_s, sx_s = late_s[:, 0:N], late_s[:, N : 2 * N], late_s[:, 2 * N :]
+        nc.vector.memset(xt_s[:].bitcast(I32), 0)
+        nc.vector.memset(w_s[:].bitcast(I32), 0)
+        nc.gpsimd.memset(xo_s[:].bitcast(I32), 0)
+        nc.vector.memset(late_s[:].bitcast(I32), 0)
+
+        def rows(queue, plane, src, q):
+            queue.dma_start(plane[32 * q : 32 * q + 4, :].bitcast(I32), src[0, 4 * q : 4 * q + 4, :].bitcast(I32))
+
+        l1 = load_list("l1", offs)
+        w_w = load_words(nc.scalar, "w_w", w_words[0])
+        rows(nc.sync, xt_s, xt_scales, 0)
+        rows(nc.scalar, xt_s, xt_scales, 1)
+        rows(nc.sync, xt_s, xt_scales, 2)
+        xt_w = load_words(nc.scalar, "xt_w", xt_words[0].rearrange("p n t -> p (n t)"))
+        rows(nc.sync, xt_s, xt_scales, 3)
+        rows(nc.scalar, w_s, w_scales, 0)
+        rows(nc.sync, w_s, w_scales, 1)
+        rows(nc.scalar, w_s, w_scales, 2)
+        rows(nc.sync, w_s, w_scales, 3)
+        xo_w = load_words(nc.scalar, "xo_w", xo_words[0].rearrange("p n t -> p (n t)"))
+        l2 = load_list("l2", offs2)
+        l3 = load_list("l3", offs3)
+        rows(nc.sync, xo_s, xo_scales, 0)
+        for q in (1, 2, 3):
+            rows(nc.gpsimd, xo_s, xo_scales, q)
+        l4 = load_list("l4", offs4)
+        tz_sb = []
+        for h in range(2):
+            t = tile(f"tz{h}", [P, E], F32)
+            nc.sync.dma_start(t[:], tz[P * h : P * (h + 1), :])
+            tz_sb.append(t)
+        l5 = load_list("l5", offs5)
+        so_sb = tile("so_sb", [P, 2], F32)
+        bo_sb = tile("bo_sb", [P, 2], F32)
+        with nc.allow_non_contiguous_dma(reason="one value a partition"):
+            nc.sync.dma_start(so_sb[:], so.rearrange("(h p) o -> p (h o)", p=P))
+            nc.sync.dma_start(bo_sb[:], bo.rearrange("(h p) o -> p (h o)", p=P))
+        ws_w = load_words(nc.sync, "ws_w", ws_words[0])
+        sx_w = load_words(nc.sync, "sx_w", sx_words[0].rearrange("p n t -> p (n t)"))
+        wb_w = load_words(nc.sync, "wb_w", wb_words[0])
+        for q in range(4):
+            rows(nc.gpsimd, ws_s, ws_scales, q)
+        for q in range(4):
+            rows(nc.sync, sx_s, sx_scales, q)
+        for q in range(4):
+            rows(nc.sync, wb_s, wb_scales, q)
+
+        wp_s = tile("wp_s", [P, 4, P], U8)
+        wp_w = tile("wp_w", [P, 4, P], U16)
+
+        xg_w = tile("xg_w", [P, J], U32)
+        xg_s = tile("xg_s", [P, J], U8)
+        og_w = tile("og_w", [P, J], U32)
+        og_s = tile("og_s", [P, J], U8)
+        nc.vector.tensor_copy(wp_w[:], w_w[:].bitcast(U16).rearrange("p (m t) -> p t m", t=4))
+        nc.vector.tensor_copy(xg_s[:], xt_s[:].indirect(l1[:]))
+        nc.vector.tensor_copy(xg_w[:], xt_w[:].indirect(l1[:]))
+        nc.vector.tensor_copy(wp_s[:], w_s[:].rearrange("p (m t) -> p t m", t=4))
+        nc.vector.tensor_copy(og_w[:], xo_w[:].indirect(l2[:]))
+        nc.vector.tensor_copy(og_s[:], xo_s[:].indirect(l2[:]))
+
+        pa = [ps.tile([P, J], F32, name=f"pa{t}", tag=f"pa{t}") for t in range(4)]
+        pb = [ps.tile([P, J], F32, name=f"pb{t}", tag=f"pb{t}") for t in range(4)]
+        for bank, gw, gs, fmt in ((pa, xg_w, xg_s, E5M2), (pb, og_w, og_s, E4M3)):
+            for t in range(4):
+                nc.tensor.matmul_mx(
+                    out=bank[t][:], lhsT=wp_w[:, t, :].bitcast(E2M1), lhsT_scale=wp_s[:, t, :],
+                    rhs=gw[:].bitcast(fmt), rhs_scale=gs[:], start=True, stop=True,
+                )
+
+        a_sb = [tile(f"a{t}", [P, J], F32) for t in range(4)]
+        b_sb = [tile(f"b{t}", [P, J], F32) for t in range(4)]
+        ag = [tile(f"ag{t}", [P, O], F32) for t in range(4)]
+        d = [tile(f"d{u}", [P, 2, O], F32) for u in range(2)]
+        hid = tile("hid", [P, O, 4], BF16)
+
+        def pick_a(t):
+            nc.scalar.activation(ag[t][:], a_sb[t][:].indirect(l3[:]), ACT.Copy)
+
+        def sub_b(t):
+            nc.vector.tensor_tensor(d[t // 2][:, t % 2, :], b_sb[t][:].indirect(l4[:]), ag[t][:], ALU.subtract)
+
+        nc.scalar.copy(a_sb[0][:], pa[0][:])
+        nc.scalar.copy(a_sb[1][:], pa[1][:])
+        pick_a(0)
+        nc.scalar.copy(a_sb[2][:], pa[2][:])
+        nc.vector.tensor_copy(a_sb[3][:], pa[3][:])
+        pick_a(1)
+        pick_a(2)
+        pick_a(3)
+        nc.vector.tensor_copy(b_sb[0][:], pb[0][:])
+        nc.vector.tensor_copy(b_sb[1][:], pb[1][:])
+        nc.scalar.copy(b_sb[2][:], pb[2][:])
+        nc.scalar.copy(b_sb[3][:], pb[3][:])
+        for t in range(4):
+            sub_b(t)
+
+        gate = []
+        for u in range(2):
+            nc.scalar.activation(hid[:, :, 2 * u : 2 * u + 2], d[u][:].rearrange("p t o -> p o t"), ACT.Abs)
+            g = tile(f"gate{u}", [P, O], F32, tag=f"d{u}")
+            nc.scalar.activation(g[:], tz_sb[u][:].indirect(l5[:]), ACT.Sigmoid, bias=bo_sb[:, u : u + 1], scale=so_sb[:, u : u + 1])
+            gate.append(g)
+
+        hq_w = tile("hq_w", [P, O], U32)
+        hq_s = tile("hq_s", [P, O], U8)
+        nc.vector.quantize_mx(out=hq_w[:].bitcast(E4M3), scales=hq_s[:], in_=hid[:].rearrange("p o t -> p (o t)"))
+
+        pp = [ps.tile([P, O], F32, name=f"pp{h}", tag=f"pb{h}") for h in range(2)]
+        for h in range(2):
+            nc.tensor.matmul_mx(
+                out=pp[h][:], lhsT=ws_w[:, 64 * h : 64 * (h + 1)].bitcast(E2M1), lhsT_scale=ws_s[:, P * h : P * (h + 1)],
+                rhs=sx_w[:].bitcast(E4M3), rhs_scale=sx_s, start=True, stop=False,
+            )
+        for h in range(2):
+            nc.tensor.matmul_mx(
+                out=pp[h][:], lhsT=wb_w[:, 64 * h : 64 * (h + 1)].bitcast(E2M1), lhsT_scale=wb_s[:, P * h : P * (h + 1)],
+                rhs=hq_w[:].bitcast(E4M3), rhs_scale=hq_s[:], start=False, stop=True,
+            )
+        for h, queue in enumerate((nc.sync, nc.scalar)):
+            y = tile(f"y{h}", [P, O], F32)
+            nc.vector.tensor_tensor(y[:], pp[h][:], gate[h][:], ALU.mult)
+            queue.dma_start(out[P * h : P * (h + 1), :], y[:])

@@ -47,31 +47,35 @@ def tile_list_oneforboth_looked_skip_finalgate_kernel(
         w_s = tile("w_s", [P, R], U8)
         late_s = tile("late_s", [P, 2 * N + O], U8)
         wb_s, ws_s, sx_s = late_s[:, 0:N], late_s[:, N : 2 * N], late_s[:, 2 * N :]
-        nc.vector.memset(xt_s[:].bitcast(I32), 0)
-        nc.vector.memset(w_s[:].bitcast(I32), 0)
-        nc.gpsimd.memset(xo_s[:].bitcast(I32), 0)
-        nc.vector.memset(late_s[:].bitcast(I32), 0)
+        for plane in (xt_s, xo_s, w_s, late_s):
+            nc.vector.memset(plane[:].bitcast(I32), 0)
 
         def rows(queue, plane, src, q):
             queue.dma_start(plane[32 * q : 32 * q + 4, :].bitcast(I32), src[0, 4 * q : 4 * q + 4, :].bitcast(I32))
+
+        def three_quadrants(plane, src):
+            words = src[0, 0:14, :].bitcast(I32)
+            nc.gpsimd.dma_start(plane[0:70, :].bitcast(I32), words.unsqueeze(0).to_broadcast([5, 14, words.shape[1]]))
 
         l1 = load_list("l1", offs)
         w_w = load_words(nc.scalar, "w_w", w_words[0])
         rows(nc.sync, xt_s, xt_scales, 0)
         rows(nc.scalar, xt_s, xt_scales, 1)
         rows(nc.sync, xt_s, xt_scales, 2)
+        rows(nc.scalar, xt_s, xt_scales, 3)
+        rows(nc.sync, w_s, w_scales, 0)
         xt_w = load_words(nc.scalar, "xt_w", xt_words[0].rearrange("p n t -> p (n t)"))
-        rows(nc.sync, xt_s, xt_scales, 3)
-        rows(nc.scalar, w_s, w_scales, 0)
         rows(nc.sync, w_s, w_scales, 1)
-        rows(nc.scalar, w_s, w_scales, 2)
-        rows(nc.sync, w_s, w_scales, 3)
+        rows(nc.sync, w_s, w_scales, 2)
         xo_w = load_words(nc.scalar, "xo_w", xo_words[0].rearrange("p n t -> p (n t)"))
+        warm_in = tile("warm_in", [P, 1], F32)
+        warm_out = tile("warm_out", [P, 1], F32)
+        nc.vector.memset(warm_in[:], 0.0)
+        nc.scalar.activation(warm_out[:], warm_in[:], ACT.Sigmoid)
+        rows(nc.sync, w_s, w_scales, 3)
         l2 = load_list("l2", offs2)
+        rows(nc.sync, xo_s, xo_scales, 3)
         l3 = load_list("l3", offs3)
-        rows(nc.sync, xo_s, xo_scales, 0)
-        for q in (1, 2, 3):
-            rows(nc.gpsimd, xo_s, xo_scales, q)
         l4 = load_list("l4", offs4)
         tz_sb = []
         for h in range(2):
@@ -87,14 +91,15 @@ def tile_list_oneforboth_looked_skip_finalgate_kernel(
         ws_w = load_words(nc.sync, "ws_w", ws_words[0])
         sx_w = load_words(nc.sync, "sx_w", sx_words[0].rearrange("p n t -> p (n t)"))
         wb_w = load_words(nc.sync, "wb_w", wb_words[0])
-        for q in range(4):
-            rows(nc.gpsimd, ws_s, ws_scales, q)
-        for q in range(4):
-            rows(nc.sync, sx_s, sx_scales, q)
-        for q in range(4):
-            rows(nc.sync, wb_s, wb_scales, q)
+        rows(nc.sync, ws_s, ws_scales, 3)
+        rows(nc.sync, sx_s, sx_scales, 3)
+        rows(nc.sync, wb_s, wb_scales, 3)
+        three_quadrants(xo_s, xo_scales)
+        three_quadrants(ws_s, ws_scales)
+        three_quadrants(sx_s, sx_scales)
+        three_quadrants(wb_s, wb_scales)
 
-        wp_s = tile("wp_s", [P, 4, P], U8)
+        wp_s = [tile(f"wp_s{u}", [P, 2, P], U8) for u in range(2)]
         wp_w = tile("wp_w", [P, 4, P], U16)
 
         xg_w = tile("xg_w", [P, J], U32)
@@ -104,16 +109,17 @@ def tile_list_oneforboth_looked_skip_finalgate_kernel(
         nc.vector.tensor_copy(wp_w[:], w_w[:].bitcast(U16).rearrange("p (m t) -> p t m", t=4))
         nc.vector.tensor_copy(xg_s[:], xt_s[:].indirect(l1[:]))
         nc.vector.tensor_copy(xg_w[:], xt_w[:].indirect(l1[:]))
-        nc.vector.tensor_copy(wp_s[:], w_s[:].rearrange("p (m t) -> p t m", t=4))
-        nc.vector.tensor_copy(og_w[:], xo_w[:].indirect(l2[:]))
+        for u in range(2):
+            nc.vector.tensor_copy(wp_s[u][:], w_s[:].rearrange("p (m t) -> p t m", t=4)[:, 2 * u : 2 * u + 2, :])
         nc.vector.tensor_copy(og_s[:], xo_s[:].indirect(l2[:]))
+        nc.vector.tensor_copy(og_w[:], xo_w[:].indirect(l2[:]))
 
         pa = [ps.tile([P, J], F32, name=f"pa{t}", tag=f"pa{t}") for t in range(4)]
         pb = [ps.tile([P, J], F32, name=f"pb{t}", tag=f"pb{t}") for t in range(4)]
         for bank, gw, gs, fmt in ((pa, xg_w, xg_s, E5M2), (pb, og_w, og_s, E4M3)):
             for t in range(4):
                 nc.tensor.matmul_mx(
-                    out=bank[t][:], lhsT=wp_w[:, t, :].bitcast(E2M1), lhsT_scale=wp_s[:, t, :],
+                    out=bank[t][:], lhsT=wp_w[:, t, :].bitcast(E2M1), lhsT_scale=wp_s[t // 2][:, t % 2, :],
                     rhs=gw[:].bitcast(fmt), rhs_scale=gs[:], start=True, stop=True,
                 )
 
@@ -129,18 +135,13 @@ def tile_list_oneforboth_looked_skip_finalgate_kernel(
         def sub_b(t):
             nc.vector.tensor_tensor(d[t // 2][:, t % 2, :], b_sb[t][:].indirect(l4[:]), ag[t][:], ALU.subtract)
 
-        nc.scalar.copy(a_sb[0][:], pa[0][:])
-        nc.scalar.copy(a_sb[1][:], pa[1][:])
-        pick_a(0)
-        nc.scalar.copy(a_sb[2][:], pa[2][:])
-        nc.vector.tensor_copy(a_sb[3][:], pa[3][:])
-        pick_a(1)
-        pick_a(2)
-        pick_a(3)
+        for t in range(4):
+            nc.scalar.copy(a_sb[t][:], pa[t][:])
+        nc.vector.tensor_copy(ag[0][:], a_sb[0][:].indirect(l3[:]))
         nc.vector.tensor_copy(b_sb[0][:], pb[0][:])
-        nc.vector.tensor_copy(b_sb[1][:], pb[1][:])
-        nc.scalar.copy(b_sb[2][:], pb[2][:])
-        nc.scalar.copy(b_sb[3][:], pb[3][:])
+        for t in (1, 2, 3):
+            pick_a(t)
+            nc.scalar.copy(b_sb[t][:], pb[t][:])
         for t in range(4):
             sub_b(t)
 

@@ -47,34 +47,41 @@ def tile_list_oneforboth_looked_skip_finalgate_kernel(
         w_s = tile("w_s", [P, R], U8)
         late_s = tile("late_s", [P, 2 * N + O], U8)
         wb_s, ws_s, sx_s = late_s[:, 0:N], late_s[:, N : 2 * N], late_s[:, 2 * N :]
-        for plane in (xt_s, xo_s, w_s, late_s):
+        for plane in (w_s, xo_s, late_s):
             nc.vector.memset(plane[:].bitcast(I32), 0)
 
         def rows(queue, plane, src, q):
             queue.dma_start(plane[32 * q : 32 * q + 4, :].bitcast(I32), src[0, 4 * q : 4 * q + 4, :].bitcast(I32))
 
+        def fill(queue, plane, src, q):
+            words = src[0, 4 * q : 4 * q + 4, :].bitcast(I32)
+            queue.dma_start(plane[32 * q : 32 * q + 32, :].bitcast(I32), words.unsqueeze(0).to_broadcast([8, 4, words.shape[1]]))
+
         def three_quadrants(plane, src):
             words = src[0, 0:14, :].bitcast(I32)
-            nc.gpsimd.dma_start(plane[0:70, :].bitcast(I32), words.unsqueeze(0).to_broadcast([5, 14, words.shape[1]]))
+            nc.scalar.dma_start(plane[0:70, :].bitcast(I32), words.unsqueeze(0).to_broadcast([5, 14, words.shape[1]]))
 
         l1 = load_list("l1", offs)
         w_w = load_words(nc.scalar, "w_w", w_words[0])
-        rows(nc.sync, xt_s, xt_scales, 0)
-        rows(nc.scalar, xt_s, xt_scales, 1)
-        rows(nc.sync, xt_s, xt_scales, 2)
-        rows(nc.scalar, xt_s, xt_scales, 3)
+        fill(nc.sync, xt_s, xt_scales, 0)
+        fill(nc.scalar, xt_s, xt_scales, 1)
+        fill(nc.sync, xt_s, xt_scales, 2)
+        fill(nc.scalar, xt_s, xt_scales, 3)
         rows(nc.sync, w_s, w_scales, 0)
         xt_w = load_words(nc.scalar, "xt_w", xt_words[0].rearrange("p n t -> p (n t)"))
-        rows(nc.sync, w_s, w_scales, 1)
-        rows(nc.sync, w_s, w_scales, 2)
-        xo_w = load_words(nc.scalar, "xo_w", xo_words[0].rearrange("p n t -> p (n t)"))
         warm_in = tile("warm_in", [P, 1], F32)
         warm_out = tile("warm_out", [P, 1], F32)
         nc.vector.memset(warm_in[:], 0.0)
         nc.scalar.activation(warm_out[:], warm_in[:], ACT.Sigmoid)
-        rows(nc.sync, w_s, w_scales, 3)
+        for q in (1, 2, 3):
+            rows(nc.sync, w_s, w_scales, q)
         l2 = load_list("l2", offs2)
-        rows(nc.sync, xo_s, xo_scales, 3)
+        xo_w = load_words(nc.scalar, "xo_w", xo_words[0].rearrange("p n t -> p (n t)"))
+        for q in (0, 1, 2):
+            rows(nc.sync, xo_s, xo_scales, q)
+        rows(nc.gpsimd, xo_s, xo_scales, 3)
+        three_quadrants(ws_s, ws_scales)
+        three_quadrants(sx_s, sx_scales)
         l3 = load_list("l3", offs3)
         l4 = load_list("l4", offs4)
         tz_sb = []
@@ -90,14 +97,13 @@ def tile_list_oneforboth_looked_skip_finalgate_kernel(
             nc.sync.dma_start(bo_sb[:], bo.rearrange("(h p) o -> p (h o)", p=P))
         ws_w = load_words(nc.sync, "ws_w", ws_words[0])
         sx_w = load_words(nc.sync, "sx_w", sx_words[0].rearrange("p n t -> p (n t)"))
-        wb_w = load_words(nc.sync, "wb_w", wb_words[0])
         rows(nc.sync, ws_s, ws_scales, 3)
         rows(nc.sync, sx_s, sx_scales, 3)
-        rows(nc.sync, wb_s, wb_scales, 3)
-        three_quadrants(xo_s, xo_scales)
-        three_quadrants(ws_s, ws_scales)
-        three_quadrants(sx_s, sx_scales)
-        three_quadrants(wb_s, wb_scales)
+        wb_w = load_words(nc.sync, "wb_w", wb_words[0])
+        for q in (0, 1):
+            rows(nc.gpsimd, wb_s, wb_scales, q)
+        for q in (2, 3):
+            rows(nc.sync, wb_s, wb_scales, q)
 
         wp_s = [tile(f"wp_s{u}", [P, 2, P], U8) for u in range(2)]
         wp_w = tile("wp_w", [P, 4, P], U16)
@@ -111,8 +117,8 @@ def tile_list_oneforboth_looked_skip_finalgate_kernel(
         nc.vector.tensor_copy(xg_w[:], xt_w[:].indirect(l1[:]))
         for u in range(2):
             nc.vector.tensor_copy(wp_s[u][:], w_s[:].rearrange("p (m t) -> p t m", t=4)[:, 2 * u : 2 * u + 2, :])
-        nc.vector.tensor_copy(og_s[:], xo_s[:].indirect(l2[:]))
         nc.vector.tensor_copy(og_w[:], xo_w[:].indirect(l2[:]))
+        nc.vector.tensor_copy(og_s[:], xo_s[:].indirect(l2[:]))
 
         pa = [ps.tile([P, J], F32, name=f"pa{t}", tag=f"pa{t}") for t in range(4)]
         pb = [ps.tile([P, J], F32, name=f"pb{t}", tag=f"pb{t}") for t in range(4)]

from contextlib import ExitStack

import concourse.mybir as mybir

K, T, Z, J, R, O, N, L, E = 512, 1024, 1024, 256, 512, 128, 256, 512, 512
FLOPS = 2 * (2 * K * R * J + R * N * O + L * N * O)

F32 = mybir.dt.float32
BF16 = mybir.dt.bfloat16
I32 = mybir.dt.int32
U32 = mybir.dt.uint32
U16 = mybir.dt.uint16
U8 = mybir.dt.uint8
E4M3 = mybir.dt.float8_e4m3fn_x4
E5M2 = mybir.dt.float8_e5m2_x4
E2M1 = mybir.dt.float4_e2m1fn_x4
ACT = mybir.ActivationFunctionType
ALU = mybir.AluOpType
P = 128


def tile_list_oneforboth_looked_skip_finalgate_kernel(
    tc, xt_words, xt_scales, xo_words, xo_scales, w_words, w_scales, wb_words, wb_scales,
    sx_words, sx_scales, ws_words, ws_scales, tz, so, bo, offs, offs2, offs3, offs4, offs5, out,
):
    nc = tc.nc
    with ExitStack() as ctx:
        lists = ctx.enter_context(tc.tile_pool(name="lists", bufs=1))
        sb = ctx.enter_context(tc.tile_pool(name="sb", bufs=1))
        ps = ctx.enter_context(tc.psum_pool(name="ps", bufs=1))

        def tile(name, shape, dtype, tag=None):
            return sb.tile(shape, dtype, name=name, tag=tag or name, align_bytes=64)

        def load_list(name, src):
            t = lists.tile(list(src.shape), U16, name=name)
            nc.sync.dma_start(t[:], src)
            return t

        def load_words(queue, name, src):
            t = tile(name, [P, src.shape[1] // 4], U32)
            queue.dma_start(t[:].bitcast(I32), src.bitcast(I32))
            return t

        xt_s = tile("xt_s", [P, T], U8)
        xo_s = tile("xo_s", [P, Z], U8)
        w_s = tile("w_s", [P, R], U8)
        late_s = tile("late_s", [P, 2 * N + O], U8)
        wb_s, ws_s, sx_s = late_s[:, 0:N], late_s[:, N : 2 * N], late_s[:, 2 * N :]
        for plane in (w_s, xo_s, late_s):
            nc.vector.memset(plane[:].bitcast(I32), 0)

        def rows(queue, plane, src, q):
            queue.dma_start(plane[32 * q : 32 * q + 4, :].bitcast(I32), src[0, 4 * q : 4 * q + 4, :].bitcast(I32))

        def fill(queue, plane, src, q):
            words = src[0, 4 * q : 4 * q + 4, :].bitcast(I32)
            queue.dma_start(plane[32 * q : 32 * q + 32, :].bitcast(I32), words.unsqueeze(0).to_broadcast([8, 4, words.shape[1]]))

        def three_quadrants(plane, src):
            words = src[0, 0:14, :].bitcast(I32)
            nc.scalar.dma_start(plane[0:70, :].bitcast(I32), words.unsqueeze(0).to_broadcast([5, 14, words.shape[1]]))

        l1 = load_list("l1", offs)
        w_w = load_words(nc.scalar, "w_w", w_words[0])
        fill(nc.sync, xt_s, xt_scales, 0)
        fill(nc.scalar, xt_s, xt_scales, 1)
        fill(nc.sync, xt_s, xt_scales, 2)
        fill(nc.scalar, xt_s, xt_scales, 3)
        rows(nc.sync, w_s, w_scales, 0)
        xt_w = load_words(nc.scalar, "xt_w", xt_words[0].rearrange("p n t -> p (n t)"))
        warm_in = tile("warm_in", [P, 1], F32)
        warm_out = tile("warm_out", [P, 1], F32)
        nc.vector.memset(warm_in[:], 0.0)
        nc.scalar.activation(warm_out[:], warm_in[:], ACT.Sigmoid)
        for q in (1, 2, 3):
            rows(nc.sync, w_s, w_scales, q)
        l2 = load_list("l2", offs2)
        xo_w = load_words(nc.scalar, "xo_w", xo_words[0].rearrange("p n t -> p (n t)"))
        for q in (0, 1, 2):
            rows(nc.sync, xo_s, xo_scales, q)
        rows(nc.gpsimd, xo_s, xo_scales, 3)
        three_quadrants(ws_s, ws_scales)
        three_quadrants(sx_s, sx_scales)
        l3 = load_list("l3", offs3)
        l4 = load_list("l4", offs4)
        tz_sb = []
        for h in range(2):
            t = tile(f"tz{h}", [P, E], F32)
            nc.sync.dma_start(t[:], tz[P * h : P * (h + 1), :])
            tz_sb.append(t)
        l5 = load_list("l5", offs5)
        so_sb = tile("so_sb", [P, 2], F32)
        bo_sb = tile("bo_sb", [P, 2], F32)
        with nc.allow_non_contiguous_dma(reason="one value a partition"):
            nc.sync.dma_start(so_sb[:], so.rearrange("(h p) o -> p (h o)", p=P))
            nc.sync.dma_start(bo_sb[:], bo.rearrange("(h p) o -> p (h o)", p=P))
        ws_w = load_words(nc.sync, "ws_w", ws_words[0])
        sx_w = load_words(nc.sync, "sx_w", sx_words[0].rearrange("p n t -> p (n t)"))
        rows(nc.sync, ws_s, ws_scales, 3)
        rows(nc.sync, sx_s, sx_scales, 3)
        wb_w = load_words(nc.sync, "wb_w", wb_words[0])
        for q in (0, 1):
            rows(nc.gpsimd, wb_s, wb_scales, q)
        for q in (2, 3):
            rows(nc.sync, wb_s, wb_scales, q)

        wp_s = [tile(f"wp_s{u}", [P, 2, P], U8) for u in range(2)]
        wp_w = tile("wp_w", [P, 4, P], U16)

        xg_w = tile("xg_w", [P, J], U32)
        xg_s = tile("xg_s", [P, J], U8)
        og_w = tile("og_w", [P, J], U32)
        og_s = tile("og_s", [P, J], U8)
        nc.vector.tensor_copy(wp_w[:], w_w[:].bitcast(U16).rearrange("p (m t) -> p t m", t=4))
        nc.vector.tensor_copy(xg_s[:], xt_s[:].indirect(l1[:]))
        nc.vector.tensor_copy(xg_w[:], xt_w[:].indirect(l1[:]))
        for u in range(2):
            nc.vector.tensor_copy(wp_s[u][:], w_s[:].rearrange("p (m t) -> p t m", t=4)[:, 2 * u : 2 * u + 2, :])
        nc.vector.tensor_copy(og_w[:], xo_w[:].indirect(l2[:]))
        nc.vector.tensor_copy(og_s[:], xo_s[:].indirect(l2[:]))

        pa = [ps.tile([P, J], F32, name=f"pa{t}", tag=f"pa{t}") for t in range(4)]
        pb = [ps.tile([P, J], F32, name=f"pb{t}", tag=f"pb{t}") for t in range(4)]
        for bank, gw, gs, fmt in ((pa, xg_w, xg_s, E5M2), (pb, og_w, og_s, E4M3)):
            for t in range(4):
                nc.tensor.matmul_mx(
                    out=bank[t][:], lhsT=wp_w[:, t, :].bitcast(E2M1), lhsT_scale=wp_s[t // 2][:, t % 2, :],
                    rhs=gw[:].bitcast(fmt), rhs_scale=gs[:], start=True, stop=True,
                )

        a_sb = [tile(f"a{t}", [P, J], F32) for t in range(4)]
        b_sb = [tile(f"b{t}", [P, J], F32) for t in range(4)]
        ag = [tile(f"ag{t}", [P, O], F32) for t in range(4)]
        d = [tile(f"d{u}", [P, 2, O], F32) for u in range(2)]
        hid = tile("hid", [P, O, 4], BF16)

        def pick_a(t):
            nc.scalar.activation(ag[t][:], a_sb[t][:].indirect(l3[:]), ACT.Copy)

        def sub_b(t):
            nc.vector.tensor_tensor(d[t // 2][:, t % 2, :], b_sb[t][:].indirect(l4[:]), ag[t][:], ALU.subtract)

        for t in range(4):
            nc.scalar.copy(a_sb[t][:], pa[t][:])
        nc.vector.tensor_copy(ag[0][:], a_sb[0][:].indirect(l3[:]))
        nc.vector.tensor_copy(b_sb[0][:], pb[0][:])
        for t in (1, 2, 3):
            pick_a(t)
            nc.scalar.copy(b_sb[t][:], pb[t][:])
        for t in range(4):
            sub_b(t)

        gate = []
        for u in range(2):
            nc.scalar.activation(hid[:, :, 2 * u : 2 * u + 2], d[u][:].rearrange("p t o -> p o t"), ACT.Abs)
            g = tile(f"gate{u}", [P, O], F32, tag=f"d{u}")
            nc.scalar.activation(g[:], tz_sb[u][:].indirect(l5[:]), ACT.Sigmoid, bias=bo_sb[:, u : u + 1], scale=so_sb[:, u : u + 1])
            gate.append(g)

        hq_w = tile("hq_w", [P, O], U32)
        hq_s = tile("hq_s", [P, O], U8)
        nc.vector.quantize_mx(out=hq_w[:].bitcast(E4M3), scales=hq_s[:], in_=hid[:].rearrange("p o t -> p (o t)"))

        pp = [ps.tile([P, O], F32, name=f"pp{h}", tag=f"pb{h}") for h in range(2)]
        for h in range(2):
            nc.tensor.matmul_mx(
                out=pp[h][:], lhsT=ws_w[:, 64 * h : 64 * (h + 1)].bitcast(E2M1), lhsT_scale=ws_s[:, P * h : P * (h + 1)],
                rhs=sx_w[:].bitcast(E4M3), rhs_scale=sx_s, start=True, stop=False,
            )
        for h in range(2):
            nc.tensor.matmul_mx(
                out=pp[h][:], lhsT=wb_w[:, 64 * h : 64 * (h + 1)].bitcast(E2M1), lhsT_scale=wb_s[:, P * h : P * (h + 1)],
                rhs=hq_w[:].bitcast(E4M3), rhs_scale=hq_s[:], start=False, stop=True,
            )
        for h, queue in enumerate((nc.sync, nc.scalar)):
            y = tile(f"y{h}", [P, O], F32)
            nc.vector.tensor_tensor(y[:], pp[h][:], gate[h][:], ALU.mult)
            queue.dma_start(out[P * h : P * (h + 1), :], y[:])
